import numpy as np, ml_dtypes
CORES = [2,42,66,74,82,90,114]
N = 7
DEG, TK, TIMES = 7, 128, 2
MASK = [[0,1,2,3,4,5,6],[0,1,2,3,4,5,6],[0,1,2,3,4,5,6],[0,1,2,3,4,5,6],[0,1,2,3,4,5,6],[0,1,2,3,4,5,6],[0,1,2,3,4,5,6]]
def setup_inputs(rng):
    return {"x": rng.standard_normal((N, 128, TK), dtype=np.float32).astype(ml_dtypes.bfloat16), "w": (rng.standard_normal((N, 128, DEG * 128), dtype=np.float32) / np.float32(np.sqrt(128 * DEG / 2))).astype(ml_dtypes.bfloat16)}
def setup_inputs_big(rng):
    d = setup_inputs(rng)
    for k in ("x",): d[k] = (d[k].astype(np.float32) * 1048576.0).astype(d[k].dtype)
    return d
def setup_inputs_small(rng):
    d = setup_inputs(rng)
    for k in ("x",): d[k] = (d[k].astype(np.float32) * (1 / 1048576.0)).astype(d[k].dtype)
    return d
def setup_inputs_apart(rng):
    d = setup_inputs(rng)
    f = (10.0 ** rng.permutation(np.linspace(-1.5, 1.5, N))).astype(np.float32).reshape(N, 1, 1)
    for k in ("x",): d[k] = (d[k].astype(np.float32) * f).astype(d[k].dtype)
    return d
def reference(x, w):
    X, W = x.astype(np.float64), w.astype(np.float64)
    h = list(X)
    for _ in range(TIMES):
        h = [np.maximum(sum(W[r][:, 128 * i:128 * i + 128].T @ h[j] for i, j in enumerate(MASK[r])), 0.0) for r in range(N)]
    return {"y": np.stack(h).astype(ml_dtypes.bfloat16)}

from concourse.bass import DstId, RemoteDMATransfer
from concourse.mybir import AluOpType

NR = 7
TK = 128

SCRATCH = {
    "h0": ("sbuf", [128, NR * TK], "bfloat16"),
    "h1": ("sbuf", [128, NR * TK], "bfloat16"),
    "ws": ("sbuf", [128, NR * TK], "bfloat16"),
    "yo": ("sbuf", [128, TK], "bfloat16"),
    "zero": ("sbuf", [128, TK], "float32"),
    "p0": ("psum", [128, 512], "float32"),
    "p1": ("psum", [128, 512], "float32"),
}
SEMAPHORES = (["sx", "sw", "sz", "sh", "sy", "st", "sent", "m0", "m1"]
              + ["a0_%d" % j for j in range(NR)] + ["a1_%d" % j for j in range(NR)])


def rank_program(g, core, T, topo):
    r = T.rank_of(core)
    if r is None:
        return
    mask_tab = T.tables["MASK"]
    cores = T.cores
    n = len(cores)

    def slot(buf, j):
        return buf[:, j * TK:(j + 1) * TK]

    users = [(r + k) % n for k in range(1, n) if r in mask_tab[(r + k) % n]]
    order = [r] + [(r - k) % n for k in range(1, n)]
    terms = sorted(enumerate(mask_tab[r]), key=lambda ij: order.index(ij[1]))

    engines = topo.mask(core, cores[users[0]])
    for u in users:
        assert topo.may_write(core, cores[u])
        engines &= topo.mask(core, cores[u])
    ne = bin(engines).count("1")

    def send(buf, sem_name):
        ids = []
        for u in users:
            rid, pid, _ = topo.addr(cores[u])
            ids.append(DstId(rid=rid, pnc=pid))
        g.remote_dma_fused(
            [RemoteDMATransfer(dst_ids=ids, dma_engine_mask=engines, remote_sem=T.sem[sem_name % r],
                               srcs=[slot(buf, r)], dsts=[slot(buf, r) for _ in users], alu_op=0)],
            local_sem=T.sem.sent)

    def multiply(buf, acc, own_sem, own_val, arr_name, done):
        seen = set()
        for k, (i, j) in enumerate(terms):
            if j not in seen:
                seen.add(j)
                if j == r:
                    g.tensor.wait_ge(own_sem, own_val)
                else:
                    g.tensor.wait_ge(T.sem[arr_name % j], ne)
            g.tensor.matmul(acc[:, 0:TK], slot(T.ws, i), slot(buf, j), k == 0, k == len(terms) - 1).then_inc(done, 1)

    g.sync.dma_start(slot(T.h0, r), T.x[:]).then_inc(T.sem.sx, 16)
    g.sync.dma_start(T.ws[:], T.w[:]).then_inc(T.sem.sw, 16)

    g.wait_ge(T.sem.sx, 16)
    send(T.h0, "a0_%d")
    g.wait_ge(T.sem.sh, 1)
    send(T.h1, "a1_%d")

    g.tensor.wait_ge(T.sem.sw, 16)
    multiply(T.h0, T.p0, T.sem.sx, 16, "a0_%d", T.sem.m0)
    multiply(T.h1, T.p1, T.sem.sh, 1, "a1_%d", T.sem.m1)

    g.vector.memset(T.zero[:], 0.0).then_inc(T.sem.sz, 1)
    g.vector.wait_ge(T.sem.sz, 1)
    g.vector.wait_ge(T.sem.m0, len(terms))
    g.vector.tensor_tensor(slot(T.h1, r), T.p0[:, 0:TK], T.zero[:], AluOpType.max).then_inc(T.sem.sh, 1)
    g.vector.wait_ge(T.sem.m1, len(terms))
    g.vector.tensor_tensor(T.yo[:], T.p1[:, 0:TK], T.zero[:], AluOpType.max).then_inc(T.sem.sy, 1)

    g.sync.wait_ge(T.sem.sy, 1)
    g.sync.dma_start(T.y[:], T.yo[:]).then_inc(T.sem.st, 16)
    g.sync.wait_ge(T.sem.st, 16)

    g.wait_ge(T.sem.sent, 2 * ne)
